import numpy as np
import ml_dtypes

BF16 = ml_dtypes.bfloat16


def bf(x):
    return np.asarray(x, np.float32).astype(BF16)


def f32(x):
    return np.asarray(x, np.float32)


def f64(x):
    return np.asarray(x).astype(np.float64)


def striped(idx):
    return np.tile(idx.reshape(-1, 16).T, (8, 1))


S, K, M, N = 512, 128, 128, 128


def setup_inputs():
    return {"base": bf(np.random.standard_normal((M, S))), "x": bf(np.random.standard_normal((K, N))), "w": bf(np.random.standard_normal((K, M)) / np.sqrt(K)), "c": f32(0.2 + 0.8 * np.random.random_sample((1, S))), "offs": striped(np.random.permutation(S)[:N])}


def reference(base, x, w, c, offs):
    idx = offs[:16].T.reshape(-1)
    z = f64(base).copy()
    z[:, idx] = f64(w).T @ f64(x)
    return z * f64(c)

@@ -1,0 +1,44 @@
+import concourse.mybir as mybir
+from concourse.masks import make_identity
+
+BF16 = mybir.dt.bfloat16
+F32 = mybir.dt.float32
+U16 = mybir.dt.uint16
+MULT = mybir.AluOpType.mult
+
+FLOPS = 2 * 128 * 128 * 128 + 128 * 512
+
+
+def tile_scatter_matmul_kernel(tc, base, x, w, c, offs, out):
+    nc = tc.nc
+    features, tokens = base.shape
+    depth, picked = x.shape
+
+    with (
+        tc.tile_pool(name="sbuf", bufs=1) as sbuf,
+        tc.psum_pool(name="psum", bufs=1) as psum,
+    ):
+        base_sb = sbuf.tile([features, tokens], BF16)
+        nc.sync.dma_start(base_sb[:], base)
+        w_sb = sbuf.tile([depth, features], BF16)
+        nc.sync.dma_start(w_sb[:], w)
+        x_sb = sbuf.tile([depth, picked], BF16)
+        nc.sync.dma_start(x_sb[:], x)
+        offsets = sbuf.tile([128, picked // 16], U16)
+        nc.sync.dma_start(offsets[:], offs)
+        c_sb = sbuf.tile([features, tokens], F32)
+        nc.sync.dma_start(c_sb[:], c.rearrange("o t -> (o t)").partition_broadcast(features))
+
+        identity = sbuf.tile([features, features], BF16)
+        make_identity(nc, identity[:])
+
+        window = psum.tile([features, tokens], F32)
+        nc.tensor.matmul(window[:], identity[:], base_sb[:], start=True, stop=True)
+
+        nc.tensor.matmul(
+            window[:].indirect(offsets[:]), w_sb[:], x_sb[:], start=True, stop=True
+        )
+
+        out_sb = sbuf.tile([features, tokens], F32)
+        nc.vector.tensor_tensor(out_sb[:], window[:], c_sb[:], MULT)
+        nc.sync.dma_start(out, out_sb[:])

@@ -18,6 +18,8 @@ def tile_scatter_matmul_kernel(tc, base, x, w, c, offs, out):
         tc.tile_pool(name="sbuf", bufs=1) as sbuf,
         tc.psum_pool(name="psum", bufs=1) as psum,
     ):
+        c_row = sbuf.tile([1, tokens], F32)
+        nc.sync.dma_start(c_row[:], c)
         base_sb = sbuf.tile([features, tokens], BF16)
         nc.sync.dma_start(base_sb[:], base)
         w_sb = sbuf.tile([depth, features], BF16)
@@ -26,11 +28,16 @@ def tile_scatter_matmul_kernel(tc, base, x, w, c, offs, out):
         nc.sync.dma_start(x_sb[:], x)
         offsets = sbuf.tile([128, picked // 16], U16)
         nc.sync.dma_start(offsets[:], offs)
-        c_sb = sbuf.tile([features, tokens], F32)
-        nc.sync.dma_start(c_sb[:], c.rearrange("o t -> (o t)").partition_broadcast(features))
 
         identity = sbuf.tile([features, features], BF16)
         make_identity(nc, identity[:])
+
+        ones = sbuf.tile([1, features], F32)
+        nc.vector.memset(ones[:], 1.0)
+        c_bank = psum.tile([features, tokens], F32)
+        nc.tensor.matmul(c_bank[:], ones[:], c_row[:], start=True, stop=True)
+        c_sb = sbuf.tile([features, tokens], F32)
+        nc.vector.tensor_copy(c_sb[:], c_bank[:])
 
         window = psum.tile([features, tokens], F32)
         nc.tensor.matmul(window[:], identity[:], base_sb[:], start=True, stop=True)

import concourse.mybir as mybir
from concourse.masks import make_identity

BF16 = mybir.dt.bfloat16
F32 = mybir.dt.float32
U16 = mybir.dt.uint16
MULT = mybir.AluOpType.mult

FLOPS = 2 * 128 * 128 * 128 + 128 * 512


def tile_scatter_matmul_kernel(tc, base, x, w, c, offs, out):
    nc = tc.nc
    features, tokens = base.shape
    depth, picked = x.shape

    with (
        tc.tile_pool(name="sbuf", bufs=1) as sbuf,
        tc.psum_pool(name="psum", bufs=1) as psum,
    ):
        c_row = sbuf.tile([1, tokens], F32)
        nc.sync.dma_start(c_row[:], c)
        base_sb = sbuf.tile([features, tokens], BF16)
        nc.sync.dma_start(base_sb[:], base)
        w_sb = sbuf.tile([depth, features], BF16)
        nc.sync.dma_start(w_sb[:], w)
        x_sb = sbuf.tile([depth, picked], BF16)
        nc.sync.dma_start(x_sb[:], x)
        offsets = sbuf.tile([128, picked // 16], U16)
        nc.sync.dma_start(offsets[:], offs)

        identity = sbuf.tile([features, features], BF16)
        make_identity(nc, identity[:])

        ones = sbuf.tile([1, features], F32)
        nc.vector.memset(ones[:], 1.0)
        c_bank = psum.tile([features, tokens], F32)
        nc.tensor.matmul(c_bank[:], ones[:], c_row[:], start=True, stop=True)
        c_sb = sbuf.tile([features, tokens], F32)
        nc.vector.tensor_copy(c_sb[:], c_bank[:])

        window = psum.tile([features, tokens], F32)
        nc.tensor.matmul(window[:], identity[:], base_sb[:], start=True, stop=True)

        nc.tensor.matmul(
            window[:].indirect(offsets[:]), w_sb[:], x_sb[:], start=True, stop=True
        )

        out_sb = sbuf.tile([features, tokens], F32)
        nc.vector.tensor_tensor(out_sb[:], window[:], c_sb[:], MULT)
        nc.sync.dma_start(out, out_sb[:])
